import numpy as np
import ml_dtypes


def mxq(x, axis, fmt="e4m3"):
    dtype, down = {"e4m3": (ml_dtypes.float8_e4m3fn, 7), "e5m2": (ml_dtypes.float8_e5m2, 14)}[fmt]
    v = np.moveaxis(np.asarray(x, np.float32).astype(ml_dtypes.bfloat16).astype(np.float64), axis, -1)
    blocks = v.reshape(v.shape[:-1] + (-1, 32))
    amax = np.abs(blocks).max(-1, keepdims=True)
    byte = np.maximum(np.where(amax > 0, np.frexp(amax)[1] - 1 + 127, 0) - down, 1)
    scale = np.exp2(byte - 127.0)
    codes = (blocks / scale).astype(np.float32).astype(dtype).astype(np.float64)
    return np.moveaxis((codes * scale).reshape(v.shape), -1, axis)


WIDE = False


def mx_kscale(k):
    if not WIDE:
        return np.ones(k)
    levels = np.array([10, -10, 5, -5, 0])
    if k % 512:
        return np.exp2(np.random.permutation(np.resize(levels, k // 32))).repeat(32)
    a = np.empty((k // 512, 16))
    for p in range(k // 512):
        a[p, :8] = np.random.permutation(np.resize(levels, 8))
        for g in range(8):
            far = levels[np.abs(levels - a[p, g]) >= 10]
            a[p, g + 8] = far[np.random.randint(len(far))]
    return np.exp2(a.ravel()).repeat(32)


BF16 = ml_dtypes.bfloat16


def bf(x):
    return np.asarray(x, np.float32).astype(BF16)


def f64(x):
    return np.asarray(x).astype(np.float64)


E2M1 = np.array([0.0, 0.5, 1.0, 1.5, 2.0, 3.0, 4.0, 6.0, -0.0, -0.5, -1.0, -1.5, -2.0, -3.0, -4.0, -6.0])


def pack_weight(w, fmt):
    k, n = w.shape
    w = f64(bf(w)).reshape(k // 32, 32, n)
    amax = np.abs(w).max(1)
    if fmt == "e4m3":
        byte = np.frexp(amax)[1] - 1 + 127 - 7
    else:
        mant, ex = np.frexp(amax / 6.0)
        byte = np.where(mant > 0.5, ex, ex - 1) + 127
    byte = np.clip(np.where(amax > 0, byte, 1), 1, 254)
    scaled = (w * np.exp2(127.0 - byte)[:, None, :]).reshape(k, n).astype(np.float32)
    by_word = np.ascontiguousarray(scaled.reshape(k // 512, 128, 4, n).transpose(0, 1, 3, 2))
    if fmt == "e4m3":
        words = by_word.astype(ml_dtypes.float8_e4m3fn).view(np.uint8)
    else:
        c = by_word.astype(ml_dtypes.float4_e2m1fn).view(np.uint8) & 0xF
        words = c[..., 0::2] | (c[..., 1::2] << 4)
    return np.ascontiguousarray(words), np.ascontiguousarray(byte.astype(np.uint8).reshape(k // 512, 16, n))


def unpack_weight(words, scales, fmt):
    g, p, n, _ = words.shape
    if fmt == "e4m3":
        vals = np.ascontiguousarray(words).view(ml_dtypes.float8_e4m3fn).astype(np.float64)
    else:
        nib = np.empty((g, p, n, 4), np.uint8)
        nib[..., 0::2] = words & 0xF
        nib[..., 1::2] = words >> 4
        vals = E2M1[nib]
    vals = vals * np.repeat(np.exp2(scales.astype(np.float64) - 127.0), 8, axis=1)[..., None]
    return vals.transpose(0, 1, 3, 2).reshape(g * 512, n)
def pack4(w):
    words, scales = pack_weight(w, "e2m1")
    return words.reshape(words.shape[0], 128, -1), scales


def unpack4(words, scales):
    return unpack_weight(words.reshape(words.shape[0], 128, -1, 2), scales, "e2m1")


D, R, L = 4096, 1024, 512


def draw0():
    s = mx_kscale(D)
    t = mx_kscale(R)
    u = np.random.standard_normal((D, R)) / np.sqrt(D)
    cal = 1 + 0.1 * np.random.standard_normal(D)
    load = 0.5 + 0.5 * np.random.random(R)
    v_words, v_scales = pack4(u.T / t[:, None])
    return {"x": bf(np.random.standard_normal((D, L)) * s[:, None]),
            "g": bf(cal / s),
            "p": bf(u.T * cal / s),
            "a": bf(load * t),
            "v_words": v_words,
            "v_scales": v_scales}


def core(x, g, p, a, v_words, v_scales):
    x = f64(x)
    c = mxq(f64(p), 1, "e4m3") @ mxq(x, 0, "e4m3")
    c = c * f64(a)[:, None]
    clutter = unpack4(v_words, v_scales).T @ mxq(c, 0, "e4m3")
    return x * f64(g)[:, None] - clutter


def e4m3fn_bytes(y):
    return np.clip(np.asarray(y, np.float64), -448.0, 448.0).astype(np.float32).astype(ml_dtypes.float8_e4m3fn).view(np.uint8)


def e4m3fn_values(b):
    return np.asarray(b, np.uint8).view(ml_dtypes.float8_e4m3fn).astype(np.float64)


def setup_inputs():
    d = draw0()
    x0 = np.asarray(d['p']).astype(np.float64)
    s = (np.max(np.abs(x0), axis=(0,), keepdims=True) / 448.0).astype(np.float32)
    out = {}
    for k, v in d.items():
        if k == 'p':
            out['p_bytes'] = e4m3fn_bytes(x0 / s.astype(np.float64))
            out['p_scale'] = s
        else:
            out[k] = v
    return out


def reference(x, g, p_bytes, p_scale, a, v_words, v_scales):
    return core(x, g, e4m3fn_values(p_bytes) * p_scale.astype(np.float64), a, v_words, v_scales)

@@ -1,0 +1,284 @@
+from contextlib import ExitStack
+
+import concourse.mybir as mybir
+from concourse.masks import make_identity
+
+D, R, L = 4096, 1024, 512
+FLOPS = 4 * D * R * L
+
+F32 = mybir.dt.float32
+BF16 = mybir.dt.bfloat16
+I32 = mybir.dt.int32
+U32 = mybir.dt.uint32
+U8 = mybir.dt.uint8
+E4M3 = mybir.dt.float8_e4m3fn
+E4M3X4 = mybir.dt.float8_e4m3fn_x4
+E2M1X4 = mybir.dt.float4_e2m1fn_x4
+MULT = mybir.AluOpType.mult
+SUB = mybir.AluOpType.subtract
+COPY = mybir.ActivationFunctionType.Copy
+
+P = 128
+PACK = 4
+KP = P * PACK
+NC = D // KP
+NG = R // KP
+NT = D // P
+STEPS = 2 * NC
+
+
+def tile_stap_clutter_removal_s13_kernel(tc, x, g, p_bytes, p_scale, a, v_words, v_scales, out):
+    nc = tc.nc
+    with ExitStack() as ctx:
+        keep = ctx.enter_context(tc.tile_pool(name="keep", bufs=1))
+        work = ctx.enter_context(tc.tile_pool(name="work", bufs=3))
+        psum = ctx.enter_context(tc.psum_pool(name="psum", bufs=4))
+        ctx.enter_context(tc.manual_schedule())
+
+        ident = keep.tile([P, P], F32, name="ident")
+        make_identity(nc, ident[:])
+        vs = keep.tile([P, NG, D], U8, name="vs", align_bytes=64)
+        nc.vector.memset(vs[:].rearrange("p g n -> p (g n)").bitcast(I32), 0)
+        g_rows = keep.tile([P, P], F32, name="g_rows")
+        nc.vector.memset(g_rows[:], 0.0)
+
+        chunks = [(0, 512), (512, 1024), (1024, 2048), (2048, 4096)]
+        p_by = p_bytes.rearrange("(g m t) k -> g m t k", g=NG, t=PACK)
+        pb0, sc = [], []
+        xr = []
+
+        def load_p0(j):
+            c0, c1 = chunks[j]
+            tb = keep.tile([P, PACK, c1 - c0], U8, name="pb0_%d" % j, align_bytes=64)
+            nc.sync.dma_start(out=tb[:], in_=p_by[0][:, :, c0:c1])
+            pb0.append(tb)
+            ts = keep.tile([P, c1 - c0], F32, name="sc_%d" % j, align_bytes=64)
+            nc.sync.dma_start(out=ts[:], in_=p_scale[:, c0:c1].rearrange("o k -> (o k)").partition_broadcast(P))
+            sc.append(ts)
+
+        def load_x(c):
+            t = work.tile([P, PACK, L], BF16, name="xr_%d" % c, tag="xr", bufs=8, align_bytes=64)
+            nc.sync.dma_start(out=t[:], in_=x[KP * c : KP * (c + 1), :].rearrange("(p j) l -> p j l", j=PACK))
+            xr.append(t)
+
+        load_p0(0)
+        load_x(0)
+        load_p0(1)
+        load_x(1)
+        load_p0(2)
+        load_x(2)
+        load_x(3)
+        load_p0(3)
+        for c in range(4, NC):
+            load_x(c)
+        a_bf = keep.tile([P, NG, PACK], BF16, name="a_bf")
+        nc.sync.dma_start(out=a_bf[:], in_=a.rearrange("(g m t) -> m g t", g=NG, t=PACK))
+        g_bf = keep.tile([P, P], BF16, name="g_bf")
+        nc.sync.dma_start(out=g_bf[0:NT, :], in_=g.rearrange("(i p) -> i p", p=P))
+        pb1 = []
+        for t in range(PACK):
+            tb = keep.tile([P, D], U8, name="pb1_%d" % t, align_bytes=64)
+            nc.sync.dma_start(out=tb[:], in_=p_by[1][:, t, :])
+            pb1.append(tb)
+        for q in range(4):
+            nc.sync.dma_start(
+                out=vs[32 * q : 32 * q + 4, :, :].bitcast(I32),
+                in_=v_scales[:, 4 * q : 4 * q + 4, :].rearrange("g q n -> q g n").bitcast(I32),
+            )
+        vw = keep.tile([P, NG, 2 * D], U8, name="vw", align_bytes=64)
+        for gg in range(NG):
+            nc.sync.dma_start(out=vw[:, gg, :].bitcast(I32), in_=v_words[gg].bitcast(I32))
+        xn = []
+        for j in range(8):
+            t = work.tile([P, 4, L], BF16, name="xn_%d" % j, tag="xr", bufs=8, align_bytes=64)
+            nc.sync.dma_start(out=t[:], in_=x[512 * j : 512 * (j + 1), :].rearrange("(i p) l -> p i l", p=P))
+            xn.append(t)
+
+        xq = keep.tile([P, NC, L], U32, name="xq", align_bytes=64)
+        xs = keep.tile([P, NC, L], U8, name="xs", align_bytes=64)
+        hq = keep.tile([P, NG, L], U32, name="hq", align_bytes=64)
+        hs = keep.tile([P, NG, L], U8, name="hs", align_bytes=64)
+        hg1 = keep.tile([P, L, PACK], BF16, name="hg1", align_bytes=64)
+        hg0 = keep.tile([P, L, PACK], BF16, name="hg0", align_bytes=64)
+        hp0 = keep.tile([P, PACK, L], BF16, name="hp0", align_bytes=64)
+        a_f = keep.tile([P, NG * PACK], F32, name="a_f")
+        g_f = keep.tile([P, NT], F32, name="g_f")
+
+        W, TR, PG, PQ, PS, XG, ACC = {}, {}, {}, {}, {}, {}, {}
+
+        def chunk_of(c):
+            for j in range(len(chunks)):
+                if chunks[j][0] <= KP * c < chunks[j][1]:
+                    return j, KP * c - chunks[j][0]
+
+        def product(s):
+            w = work.tile([P, 4 * KP], BF16, name="w", tag="w", align_bytes=64)
+            if s < NC:
+                j, off = chunk_of(s)
+                for t in range(PACK):
+                    nc.vector.tensor_tensor(
+                        out=w[:, KP * t : KP * (t + 1)],
+                        in0=pb0[j][:, t, off : off + KP].bitcast(E4M3),
+                        in1=sc[j][:, off : off + KP],
+                        op=MULT,
+                    )
+            else:
+                t, h = (s - NC) // 2, (s - NC) % 2
+                for piece in range(2):
+                    k0 = 2048 * h + 1024 * piece
+                    if k0 < 1024:
+                        parts = [(0, 0, 0, 512), (1, 0, 512, 512)]
+                    elif k0 < 2048:
+                        parts = [(2, 0, 1024, 1024)]
+                    else:
+                        parts = [(3, k0 - 2048, k0, 1024)]
+                    for j, so, kk, n in parts:
+                        o = kk - 2048 * h
+                        nc.vector.tensor_tensor(
+                            out=w[:, o : o + n],
+                            in0=pb1[t][:, kk : kk + n].bitcast(E4M3),
+                            in1=sc[j][:, so : so + n],
+                            op=MULT,
+                        )
+            W[s] = w
+
+        def transposes(s):
+            words = W[s][:].bitcast(F32)
+            banks = []
+            for b in range(2):
+                tr = psum.tile([P, 2, 2, P], F32, name="tr", tag="tr")
+                for j in range(2):
+                    for u in range(2):
+                        k0 = 256 * (2 * b + j)
+                        nc.tensor.transpose(tr[:, j, u, :], words[:, k0 + u : k0 + 256 : 2], ident[:])
+                banks.append(tr)
+            TR[s] = banks
+
+        def evac(s):
+            pg = work.tile([P, 4, P, PACK], BF16, name="pg", tag="pg", align_bytes=64)
+            pw = pg[:].rearrange("p j m t -> p (j m t)").bitcast(F32).rearrange("p (j m u) -> p j m u", j=4, u=2)
+            for b in range(2):
+                nc.scalar.copy(
+                    out=pw[:, 2 * b : 2 * b + 2, :, :],
+                    in_=TR[s][b][:].rearrange("p j u m -> p j m u"),
+                )
+            PG[s] = pg
+
+        def quant_p(s):
+            q = work.tile([P, 4 * P], U32, name="pq", tag="pq", align_bytes=64)
+            z = work.tile([P, 4 * P], U8, name="ps", tag="ps", align_bytes=64)
+            nc.vector.quantize_mx(out=q[:].bitcast(E4M3X4), scales=z[:], in_=PG[s][:].rearrange("p j m t -> p (j m t)"))
+            PQ[s], PS[s] = q, z
+
+        def x_interleave(c):
+            t = work.tile([P, L, PACK], BF16, name="xg", tag="xg", align_bytes=64)
+            nc.scalar.copy(
+                out=t[:].rearrange("p (c i) t -> p c t i", i=4),
+                in_=xr[c][:].rearrange("p t (c i) -> p c t i", i=4),
+            )
+            XG[c] = t
+
+        def quant_x(c):
+            nc.vector.quantize_mx(
+                out=xq[:, c, :].bitcast(E4M3X4), scales=xs[:, c, :], in_=XG[c][:].rearrange("p l t -> p (l t)")
+            )
+
+        def mm(s):
+            for j in range(4):
+                if s < NC:
+                    key, c = (0, j), s
+                else:
+                    key, c = (1, (s - NC) // 2), 4 * ((s - NC) % 2) + j
+                if c == 0:
+                    ACC[key] = psum.tile([P, L], F32, name="acc", tag="acc")
+                nc.tensor.matmul_mx(
+                    out=ACC[key][:],
+                    lhsT=PQ[s][:, P * j : P * (j + 1)].bitcast(E4M3X4),
+                    lhsT_scale=PS[s][:, P * j : P * (j + 1)],
+                    rhs=xq[:, c, :].bitcast(E4M3X4),
+                    rhs_scale=xs[:, c, :],
+                    start=(c == 0),
+                    stop=(c == NC - 1),
+                )
+
+        def quant_h(gg, src):
+            nc.vector.quantize_mx(
+                out=hq[:, gg, :].bitcast(E4M3X4), scales=hs[:, gg, :], in_=src[:].rearrange("p l t -> p (l t)")
+            )
+
+        for s in range(STEPS + 2):
+            if s < STEPS:
+                product(s)
+                transposes(s)
+                if s < NC:
+                    x_interleave(s)
+                evac(s)
+            if 0 <= s - 1 < NC:
+                quant_x(s - 1)
+            if s >= 2:
+                quant_p(s - 2)
+                mm(s - 2)
+            if s == 4:
+                nc.scalar.copy(out=a_f[:], in_=a_bf[:].rearrange("p g t -> p (g t)"))
+                nc.vector.tensor_copy(out=g_rows[0:NT, :], in_=g_bf[0:NT, :])
+            if s == NC + 1:
+                for t in range(PACK):
+                    nc.scalar.activation(out=hp0[:, t, :], in_=ACC[(0, t)][:], func=COPY, scale=a_f[:, t : t + 1])
+            if s == NC + 2:
+                nc.scalar.copy(
+                    out=hg0[:].rearrange("p (c i) t -> p c t i", i=4), in_=hp0[:].rearrange("p t (c i) -> p c t i", i=4)
+                )
+            if s == NC + 3:
+                quant_h(0, hg0)
+            if s in (NC + 3, NC + 5, NC + 7):
+                t = (s - NC - 3) // 2
+                nc.scalar.activation(
+                    out=hg1[:, :, t], in_=ACC[(1, t)][:], func=COPY, scale=a_f[:, PACK + t : PACK + t + 1]
+                )
+        gt = psum.tile([P, P], F32, name="gt", tag="tr")
+        nc.tensor.transpose(gt[:], g_rows[:], ident[:])
+        nc.scalar.copy(out=g_f[:], in_=gt[:, 0:NT])
+
+        t = PACK - 1
+        nc.scalar.activation(
+            out=hg1[:, 256:, t], in_=ACC[(1, t)][:, 256:], func=COPY, scale=a_f[:, PACK + t : PACK + t + 1]
+        )
+        nc.vector.tensor_scalar(
+            out=hg1[:, :256, t], in0=ACC[(1, t)][:, :256], scalar1=a_f[:, PACK + t : PACK + t + 1], scalar2=None, op0=MULT
+        )
+        quant_h(1, hg1)
+
+        Y = {}
+
+        def y_pass(i, gg):
+            if gg == 0:
+                Y[i] = psum.tile([P, L], F32, name="y", tag="tr" if i % 8 < 4 else "acc")
+            nc.tensor.matmul_mx(
+                out=Y[i][:],
+                lhsT=vw[:, gg, 256 * i : 256 * (i + 1)].bitcast(E2M1X4),
+                lhsT_scale=vs[:, gg, P * i : P * (i + 1)],
+                rhs=hq[:, gg, :].bitcast(E4M3X4),
+                rhs_scale=hs[:, gg, :],
+                start=(gg == 0),
+                stop=(gg == NG - 1),
+            )
+
+        for i in range(7):
+            y_pass(i, 0)
+        o = None
+        for i in range(NT):
+            y_pass(i, 1)
+            if i >= 1 and i + 6 < NT:
+                y_pass(i + 6, 0)
+            if i % 2 == 0:
+                o = work.tile([P, 2, L], F32, name="o", tag="o", bufs=4, align_bytes=64)
+            nc.vector.scalar_tensor_tensor(
+                out=o[:, i % 2, :],
+                in0=xn[i // 4][:, i % 4, :],
+                scalar=g_f[:, i : i + 1],
+                in1=Y[i][:],
+                op0=MULT,
+                op1=SUB,
+            )
+            if i % 2 == 1:
+                nc.sync.dma_start(out=out[P * (i - 1) : P * (i + 1), :].rearrange("(i p) l -> p i l", p=P), in_=o[:])

@@ -24,7 +24,16 @@ KP = P * PACK
 NC = D // KP
 NG = R // KP
 NT = D // P
-STEPS = 2 * NC
+WIDE = 5
+STEPS = NC + 2 * (2 * PACK - WIDE)
+LAST = STEPS - 1
+
+
+def units_of(s):
+    if s < NC:
+        return [(r, s) for r in range(WIDE)]
+    r, h = WIDE + (s - NC) // 2, (s - NC) % 2
+    return [(r, 4 * h + j) for j in range(4)]
 
 
 def tile_stap_clutter_removal_s13_kernel(tc, x, g, p_bytes, p_scale, a, v_words, v_scales, out):
@@ -42,44 +51,53 @@ def tile_stap_clutter_removal_s13_kernel(tc, x, g, p_bytes, p_scale, a, v_words,
         g_rows = keep.tile([P, P], F32, name="g_rows")
         nc.vector.memset(g_rows[:], 0.0)
 
-        chunks = [(0, 512), (512, 1024), (1024, 2048), (2048, 4096)]
         p_by = p_bytes.rearrange("(g m t) k -> g m t k", g=NG, t=PACK)
-        pb0, sc = [], []
-        xr = []
+        sc = keep.tile([P, D], F32, name="sc", align_bytes=64)
+        pb0, pb4, xr = {}, {}, {}
 
-        def load_p0(j):
-            c0, c1 = chunks[j]
-            tb = keep.tile([P, PACK, c1 - c0], U8, name="pb0_%d" % j, align_bytes=64)
-            nc.sync.dma_start(out=tb[:], in_=p_by[0][:, :, c0:c1])
-            pb0.append(tb)
-            ts = keep.tile([P, c1 - c0], F32, name="sc_%d" % j, align_bytes=64)
-            nc.sync.dma_start(out=ts[:], in_=p_scale[:, c0:c1].rearrange("o k -> (o k)").partition_broadcast(P))
-            sc.append(ts)
+        def load_scale(c):
+            ks = slice(KP * c, KP * (c + 1))
+            nc.sync.dma_start(out=sc[:, ks], in_=p_scale[:, ks].rearrange("o k -> (o k)").partition_broadcast(P))
+
+        def load_p(c0, c1):
+            t0 = keep.tile([P, PACK, KP * (c1 - c0)], U8, name="pb0_%d" % c0, align_bytes=64)
+            nc.sync.dma_start(out=t0[:], in_=p_by[0][:, :, KP * c0 : KP * c1])
+            t4 = keep.tile([P, KP * (c1 - c0)], U8, name="pb4_%d" % c0, align_bytes=64)
+            nc.sync.dma_start(out=t4[:], in_=p_by[1][:, 0, KP * c0 : KP * c1])
+            for c in range(c0, c1):
+                pb0[c] = (t0, KP * (c - c0))
+                pb4[c] = (t4, KP * (c - c0))
 
         def load_x(c):
             t = work.tile([P, PACK, L], BF16, name="xr_%d" % c, tag="xr", bufs=8, align_bytes=64)
             nc.sync.dma_start(out=t[:], in_=x[KP * c : KP * (c + 1), :].rearrange("(p j) l -> p j l", j=PACK))
-            xr.append(t)
+            xr[c] = t
 
-        load_p0(0)
+        load_scale(0)
+        load_p(0, 1)
         load_x(0)
-        load_p0(1)
+        load_scale(1)
+        load_p(1, 2)
         load_x(1)
-        load_p0(2)
+        load_scale(2)
+        load_p(2, 4)
         load_x(2)
+        load_scale(3)
         load_x(3)
-        load_p0(3)
+        load_scale(4)
+        load_p(4, 8)
         for c in range(4, NC):
             load_x(c)
+            if c + 1 < NC:
+                load_scale(c + 1)
         a_bf = keep.tile([P, NG, PACK], BF16, name="a_bf")
         nc.sync.dma_start(out=a_bf[:], in_=a.rearrange("(g m t) -> m g t", g=NG, t=PACK))
         g_bf = keep.tile([P, P], BF16, name="g_bf")
         nc.sync.dma_start(out=g_bf[0:NT, :], in_=g.rearrange("(i p) -> i p", p=P))
-        pb1 = []
-        for t in range(PACK):
-            tb = keep.tile([P, D], U8, name="pb1_%d" % t, align_bytes=64)
-            nc.sync.dma_start(out=tb[:], in_=p_by[1][:, t, :])
-            pb1.append(tb)
+        pb1 = {}
+        for r in range(WIDE, 2 * PACK):
+            pb1[r] = keep.tile([P, D], U8, name="pb1_%d" % r, align_bytes=64)
+            nc.sync.dma_start(out=pb1[r][:], in_=p_by[1][:, r - PACK, :])
         for q in range(4):
             nc.sync.dma_start(
                 out=vs[32 * q : 32 * q + 4, :, :].bitcast(I32),
@@ -106,93 +124,76 @@ def tile_stap_clutter_removal_s13_kernel(tc, x, g, p_bytes, p_scale, a, v_words,
 
         W, TR, PG, PQ, PS, XG, ACC = {}, {}, {}, {}, {}, {}, {}
 
-        def chunk_of(c):
-            for j in range(len(chunks)):
-                if chunks[j][0] <= KP * c < chunks[j][1]:
-                    return j, KP * c - chunks[j][0]
-
-        def product(s):
-            w = work.tile([P, 4 * KP], BF16, name="w", tag="w", align_bytes=64)
-            if s < NC:
-                j, off = chunk_of(s)
-                for t in range(PACK):
-                    nc.vector.tensor_tensor(
-                        out=w[:, KP * t : KP * (t + 1)],
-                        in0=pb0[j][:, t, off : off + KP].bitcast(E4M3),
-                        in1=sc[j][:, off : off + KP],
-                        op=MULT,
-                    )
-            else:
-                t, h = (s - NC) // 2, (s - NC) % 2
-                for piece in range(2):
-                    k0 = 2048 * h + 1024 * piece
-                    if k0 < 1024:
-                        parts = [(0, 0, 0, 512), (1, 0, 512, 512)]
-                    elif k0 < 2048:
-                        parts = [(2, 0, 1024, 1024)]
-                    else:
-                        parts = [(3, k0 - 2048, k0, 1024)]
-                    for j, so, kk, n in parts:
-                        o = kk - 2048 * h
-                        nc.vector.tensor_tensor(
-                            out=w[:, o : o + n],
-                            in0=pb1[t][:, kk : kk + n].bitcast(E4M3),
-                            in1=sc[j][:, so : so + n],
-                            op=MULT,
-                        )
-            W[s] = w
-
-        def transposes(s):
-            words = W[s][:].bitcast(F32)
-            banks = []
-            for b in range(2):
-                tr = psum.tile([P, 2, 2, P], F32, name="tr", tag="tr")
-                for j in range(2):
-                    for u in range(2):
-                        k0 = 256 * (2 * b + j)
-                        nc.tensor.transpose(tr[:, j, u, :], words[:, k0 + u : k0 + 256 : 2], ident[:])
-                banks.append(tr)
-            TR[s] = banks
-
-        def evac(s):
-            pg = work.tile([P, 4, P, PACK], BF16, name="pg", tag="pg", align_bytes=64)
-            pw = pg[:].rearrange("p j m t -> p (j m t)").bitcast(F32).rearrange("p (j m u) -> p j m u", j=4, u=2)
-            for b in range(2):
-                nc.scalar.copy(
-                    out=pw[:, 2 * b : 2 * b + 2, :, :],
-                    in_=TR[s][b][:].rearrange("p j u m -> p j m u"),
+        def product(s, lo, hi):
+            units = units_of(s)
+            if s not in W:
+                W[s] = work.tile([P, WIDE * KP], BF16, name="w", tag="w", align_bytes=64)
+            for j in range(lo, hi):
+                r, c = units[j]
+                if r < PACK:
+                    t, off = pb0[c]
+                    src = t[:, r, off : off + KP]
+                elif r < WIDE:
+                    t, off = pb4[c]
+                    src = t[:, off : off + KP]
+                else:
+                    src = pb1[r][:, KP * c : KP * (c + 1)]
+                nc.vector.tensor_tensor(
+                    out=W[s][:, KP * j : KP * (j + 1)],
+                    in0=src.bitcast(E4M3),
+                    in1=sc[:, KP * c : KP * (c + 1)],
+                    op=MULT,
                 )
-            PG[s] = pg
 
-        def quant_p(s):
-            q = work.tile([P, 4 * P], U32, name="pq", tag="pq", align_bytes=64)
-            z = work.tile([P, 4 * P], U8, name="ps", tag="ps", align_bytes=64)
-            nc.vector.quantize_mx(out=q[:].bitcast(E4M3X4), scales=z[:], in_=PG[s][:].rearrange("p j m t -> p (j m t)"))
-            PQ[s], PS[s] = q, z
+        def transposes(s, b):
+            words = W[s][:].bitcast(F32)
+            tr = psum.tile([P, 2, 2, P], F32, name="tr", tag="tr", bufs=8 - WIDE)
+            for j in range(2 * b, min(2 * b + 2, len(units_of(s)))):
+                for u in range(2):
+                    nc.tensor.transpose(tr[:, j % 2, u, :], words[:, 256 * j + u : 256 * (j + 1) : 2], ident[:])
+            TR[(s, b)] = tr
 
-        def x_interleave(c):
-            t = work.tile([P, L, PACK], BF16, name="xg", tag="xg", align_bytes=64)
+        def evac(s, lo, hi):
+            if s not in PG:
+                PG[s] = work.tile([P, WIDE, P, PACK], BF16, name="pg", tag="pg", align_bytes=64)
+            pw = PG[s][:].rearrange("p j m t -> p (j m t)").bitcast(F32)
+            pw = pw.rearrange("p (j m u) -> p j m u", j=WIDE, u=2)
+            b = lo // 2
             nc.scalar.copy(
-                out=t[:].rearrange("p (c i) t -> p c t i", i=4),
-                in_=xr[c][:].rearrange("p t (c i) -> p c t i", i=4),
+                out=pw[:, lo:hi, :, :],
+                in_=TR[(s, b)][:, lo - 2 * b : hi - 2 * b, :, :].rearrange("p j u m -> p j m u"),
             )
-            XG[c] = t
+
+        def quant_p(s, lo, hi):
+            if s not in PQ:
+                PQ[s] = work.tile([P, WIDE * P], U32, name="pq", tag="pq", align_bytes=64)
+                PS[s] = work.tile([P, WIDE * P], U8, name="ps", tag="ps", align_bytes=64)
+            nc.vector.quantize_mx(
+                out=PQ[s][:, P * lo : P * hi].bitcast(E4M3X4),
+                scales=PS[s][:, P * lo : P * hi],
+                in_=PG[s][:, lo:hi, :, :].rearrange("p j m t -> p (j m t)"),
+            )
+
+        def x_interleave(c, lo, hi):
+            if c not in XG:
+                XG[c] = work.tile([P, L, PACK], BF16, name="xg", tag="xg", align_bytes=64)
+            nc.scalar.copy(
+                out=XG[c][:, lo:hi, :].rearrange("p (c i) t -> p c t i", i=4),
+                in_=xr[c][:, :, lo:hi].rearrange("p t (c i) -> p c t i", i=4),
+            )
 
         def quant_x(c):
             nc.vector.quantize_mx(
                 out=xq[:, c, :].bitcast(E4M3X4), scales=xs[:, c, :], in_=XG[c][:].rearrange("p l t -> p (l t)")
             )
 
-        def mm(s):
-            for j in range(4):
-                if s < NC:
-                    key, c = (0, j), s
-                else:
-                    key, c = (1, (s - NC) // 2), 4 * ((s - NC) % 2) + j
+        def mm(s, lo, hi):
+            for j in range(lo, min(hi, len(units_of(s)))):
+                r, c = units_of(s)[j]
                 if c == 0:
-                    ACC[key] = psum.tile([P, L], F32, name="acc", tag="acc")
+                    ACC[r] = psum.tile([P, L], F32, name="acc", tag="acc", bufs=WIDE)
                 nc.tensor.matmul_mx(
-                    out=ACC[key][:],
+                    out=ACC[r][:],
                     lhsT=PQ[s][:, P * j : P * (j + 1)].bitcast(E4M3X4),
                     lhsT_scale=PS[s][:, P * j : P * (j + 1)],
                     rhs=xq[:, c, :].bitcast(E4M3X4),
@@ -206,53 +207,103 @@ def tile_stap_clutter_removal_s13_kernel(tc, x, g, p_bytes, p_scale, a, v_words,
                 out=hq[:, gg, :].bitcast(E4M3X4), scales=hs[:, gg, :], in_=src[:].rearrange("p l t -> p (l t)")
             )
 
-        for s in range(STEPS + 2):
-            if s < STEPS:
-                product(s)
-                transposes(s)
-                if s < NC:
-                    x_interleave(s)
-                evac(s)
-            if 0 <= s - 1 < NC:
-                quant_x(s - 1)
+        def h0_evac(t):
+            nc.scalar.activation(out=hp0[:, t, :], in_=ACC[t][:], func=COPY, scale=a_f[:, t : t + 1])
+
+        def h0_interleave(lo, hi):
+            nc.scalar.copy(
+                out=hg0[:, lo:hi, :].rearrange("p (c i) t -> p c t i", i=4),
+                in_=hp0[:, :, lo:hi].rearrange("p t (c i) -> p c t i", i=4),
+            )
+
+        def h1_scalar(t, lo, hi):
+            r = PACK + t
+            nc.scalar.activation(out=hg1[:, lo:hi, t], in_=ACC[r][:, lo:hi], func=COPY, scale=a_f[:, r : r + 1])
+
+        def h1_vector(t, lo, hi):
+            r = PACK + t
+            nc.vector.tensor_scalar(
+                out=hg1[:, lo:hi, t], in0=ACC[r][:, lo:hi], scalar1=a_f[:, r : r + 1], scalar2=None, op0=MULT
+            )
+
+        for s in range(STEPS):
+            wide = s < NC
+            product(s, 0, 2)
+            transposes(s, 0)
+            if s == NC + 2:
+                h0_evac(0)
+            if s >= 1:
+                n = len(units_of(s - 1))
+                evac(s - 1, 4 if n > 4 else 2, n)
+            if s == NC + 2:
+                h0_evac(1)
+            if s == NC + 3:
+                h0_evac(2)
+                h0_evac(3)
+            if wide:
+                x_interleave(s, 0, 256)
+            evac_late = s == LAST
+            if evac_late:
+                evac(s, 0, 1)
+                evac(s, 1, 2)
+            else:
+                evac(s, 0, 2)
+            if wide:
+                x_interleave(s, 256, 512)
+            if s == NC + 2:
+                h1_scalar(0, 0, 256)
+            if s == NC + 3:
+                h1_scalar(0, 256, 512)
+            if s == NC + 4:
+                h0_interleave(0, 512)
+            if s == NC + 5:
+                h1_scalar(1, 0, 512)
             if s >= 2:
-                quant_p(s - 2)
-                mm(s - 2)
-            if s == 4:
+                quant_p(s - 2, 0, 4)
+                if s - 2 < NC:
+                    quant_p(s - 2, 4, 5)
+                mm(s - 2, 0, 2)
+            product(s, 2, 4)
+            transposes(s, 1)
+            if wide:
+                evac(s, 2, 4)
+            if s >= 2:
+                mm(s - 2, 2, 4)
+            if wide:
+                product(s, 4, 5)
+                transposes(s, 2)
+                if s >= 2:
+                    mm(s - 2, 4, 5)
+            elif s - 2 < NC:
+                mm(s - 2, 4, 5)
+            if 1 <= s <= NC:
+                quant_x(s - 1)
+            if s == NC + 1:
                 nc.scalar.copy(out=a_f[:], in_=a_bf[:].rearrange("p g t -> p (g t)"))
                 nc.vector.tensor_copy(out=g_rows[0:NT, :], in_=g_bf[0:NT, :])
-            if s == NC + 1:
-                for t in range(PACK):
-                    nc.scalar.activation(out=hp0[:, t, :], in_=ACC[(0, t)][:], func=COPY, scale=a_f[:, t : t + 1])
-            if s == NC + 2:
-                nc.scalar.copy(
-                    out=hg0[:].rearrange("p (c i) t -> p c t i", i=4), in_=hp0[:].rearrange("p t (c i) -> p c t i", i=4)
-                )
-            if s == NC + 3:
-                quant_h(0, hg0)
-            if s in (NC + 3, NC + 5, NC + 7):
-                t = (s - NC - 3) // 2
-                nc.scalar.activation(
-                    out=hg1[:, :, t], in_=ACC[(1, t)][:], func=COPY, scale=a_f[:, PACK + t : PACK + t + 1]
-                )
-        gt = psum.tile([P, P], F32, name="gt", tag="tr")
-        nc.tensor.transpose(gt[:], g_rows[:], ident[:])
-        nc.scalar.copy(out=g_f[:], in_=gt[:, 0:NT])
-
-        t = PACK - 1
-        nc.scalar.activation(
-            out=hg1[:, 256:, t], in_=ACC[(1, t)][:, 256:], func=COPY, scale=a_f[:, PACK + t : PACK + t + 1]
-        )
-        nc.vector.tensor_scalar(
-            out=hg1[:, :256, t], in0=ACC[(1, t)][:, :256], scalar1=a_f[:, PACK + t : PACK + t + 1], scalar2=None, op0=MULT
-        )
+        evac(LAST, 2, 3)
+        evac(LAST, 3, 4)
+        quant_p(LAST - 1, 0, 4)
+        mm(LAST - 1, 0, 4)
+        for j in range(2):
+            quant_p(LAST, j, j + 1)
+            mm(LAST, j, j + 1)
+        h1_scalar(2, 256, L)
+        quant_h(0, hg0)
+        h1_vector(2, 0, 256)
+        for j in range(2, 4):
+            quant_p(LAST, j, j + 1)
+            mm(LAST, j, j + 1)
+        h1_scalar(3, 256, L)
+        h1_vector(3, 0, 256)
         quant_h(1, hg1)
 
         Y = {}
 
         def y_pass(i, gg):
             if gg == 0:
-                Y[i] = psum.tile([P, L], F32, name="y", tag="tr" if i % 8 < 4 else "acc")
+                tr = i % 8 < 8 - WIDE
+                Y[i] = psum.tile([P, L], F32, name="y", tag="tr" if tr else "acc", bufs=8 - WIDE if tr else WIDE)
             nc.tensor.matmul_mx(
                 out=Y[i][:],
                 lhsT=vw[:, gg, 256 * i : 256 * (i + 1)].bitcast(E2M1X4),
@@ -263,22 +314,34 @@ def tile_stap_clutter_removal_s13_kernel(tc, x, g, p_bytes, p_scale, a, v_words,
                 stop=(gg == NG - 1),
             )
 
+        gt = psum.tile([P, P], F32, name="gt", tag="tr", bufs=8 - WIDE)
+        nc.tensor.transpose(gt[:], g_rows[:], ident[:])
+        nc.scalar.copy(out=g_f[:], in_=gt[:, 0:NT])
+
+        groups = [(0, 1), (1, 2)] + [(i, i + 2) for i in range(2, NT - 2, 2)] + [(NT - 2, NT - 1), (NT - 1, NT)]
+        first, end, o = {}, {}, None
+        for lo, hi in groups:
+            for i in range(lo, hi):
+                first[i], end[i] = lo, hi
+
         for i in range(7):
             y_pass(i, 0)
-        o = None
         for i in range(NT):
             y_pass(i, 1)
             if i >= 1 and i + 6 < NT:
                 y_pass(i + 6, 0)
-            if i % 2 == 0:
-                o = work.tile([P, 2, L], F32, name="o", tag="o", bufs=4, align_bytes=64)
-            nc.vector.scalar_tensor_tensor(
-                out=o[:, i % 2, :],
-                in0=xn[i // 4][:, i % 4, :],
-                scalar=g_f[:, i : i + 1],
-                in1=Y[i][:],
-                op0=MULT,
-                op1=SUB,
-            )
-            if i % 2 == 1:
-                nc.sync.dma_start(out=out[P * (i - 1) : P * (i + 1), :].rearrange("(i p) l -> p i l", p=P), in_=o[:])
+            if i == first[i]:
+                o = work.tile([P, 2, L], F32, name="o", tag="o", bufs=6, align_bytes=64)
+            xi, gi, oi = xn[i // 4][:, i % 4, :], g_f[:, i : i + 1], o[:, i - first[i], :]
+            if i % 4 == 3 and i < NT - 4:
+                gx = work.tile([P, L], F32, name="gx", tag="gx", bufs=2)
+                ys = work.tile([P, L], F32, name="ys", tag="ys", bufs=2)
+                nc.scalar.activation(out=gx[:], in_=xi, func=COPY, scale=gi)
+                nc.scalar.copy(out=ys[:], in_=Y[i][:])
+                nc.gpsimd.tensor_tensor(out=oi, in0=gx[:], in1=ys[:], op=SUB)
+            else:
+                nc.vector.scalar_tensor_tensor(out=oi, in0=xi, scalar=gi, in1=Y[i][:], op0=MULT, op1=SUB)
+            if i == end[i] - 1:
+                nc.sync.dma_start(
+                    out=out[P * first[i] : P * end[i], :].rearrange("(i p) l -> p i l", p=P), in_=o[:, 0 : end[i] - first[i], :]
+                )

from contextlib import ExitStack

import concourse.mybir as mybir
from concourse.masks import make_identity

D, R, L = 4096, 1024, 512
FLOPS = 4 * D * R * L

F32 = mybir.dt.float32
BF16 = mybir.dt.bfloat16
I32 = mybir.dt.int32
U32 = mybir.dt.uint32
U8 = mybir.dt.uint8
E4M3 = mybir.dt.float8_e4m3fn
E4M3X4 = mybir.dt.float8_e4m3fn_x4
E2M1X4 = mybir.dt.float4_e2m1fn_x4
MULT = mybir.AluOpType.mult
SUB = mybir.AluOpType.subtract
COPY = mybir.ActivationFunctionType.Copy

P = 128
PACK = 4
KP = P * PACK
NC = D // KP
NG = R // KP
NT = D // P
WIDE = 5
STEPS = NC + 2 * (2 * PACK - WIDE)
LAST = STEPS - 1


def units_of(s):
    if s < NC:
        return [(r, s) for r in range(WIDE)]
    r, h = WIDE + (s - NC) // 2, (s - NC) % 2
    return [(r, 4 * h + j) for j in range(4)]


def tile_stap_clutter_removal_s13_kernel(tc, x, g, p_bytes, p_scale, a, v_words, v_scales, out):
    nc = tc.nc
    with ExitStack() as ctx:
        keep = ctx.enter_context(tc.tile_pool(name="keep", bufs=1))
        work = ctx.enter_context(tc.tile_pool(name="work", bufs=3))
        psum = ctx.enter_context(tc.psum_pool(name="psum", bufs=4))
        ctx.enter_context(tc.manual_schedule())

        ident = keep.tile([P, P], F32, name="ident")
        make_identity(nc, ident[:])
        vs = keep.tile([P, NG, D], U8, name="vs", align_bytes=64)
        nc.vector.memset(vs[:].rearrange("p g n -> p (g n)").bitcast(I32), 0)
        g_rows = keep.tile([P, P], F32, name="g_rows")
        nc.vector.memset(g_rows[:], 0.0)

        p_by = p_bytes.rearrange("(g m t) k -> g m t k", g=NG, t=PACK)
        sc = keep.tile([P, D], F32, name="sc", align_bytes=64)
        pb0, pb4, xr = {}, {}, {}

        def load_scale(c):
            ks = slice(KP * c, KP * (c + 1))
            nc.sync.dma_start(out=sc[:, ks], in_=p_scale[:, ks].rearrange("o k -> (o k)").partition_broadcast(P))

        def load_p(c0, c1):
            t0 = keep.tile([P, PACK, KP * (c1 - c0)], U8, name="pb0_%d" % c0, align_bytes=64)
            nc.sync.dma_start(out=t0[:], in_=p_by[0][:, :, KP * c0 : KP * c1])
            t4 = keep.tile([P, KP * (c1 - c0)], U8, name="pb4_%d" % c0, align_bytes=64)
            nc.sync.dma_start(out=t4[:], in_=p_by[1][:, 0, KP * c0 : KP * c1])
            for c in range(c0, c1):
                pb0[c] = (t0, KP * (c - c0))
                pb4[c] = (t4, KP * (c - c0))

        def load_x(c):
            t = work.tile([P, PACK, L], BF16, name="xr_%d" % c, tag="xr", bufs=8, align_bytes=64)
            nc.sync.dma_start(out=t[:], in_=x[KP * c : KP * (c + 1), :].rearrange("(p j) l -> p j l", j=PACK))
            xr[c] = t

        load_scale(0)
        load_p(0, 1)
        load_x(0)
        load_scale(1)
        load_p(1, 2)
        load_x(1)
        load_scale(2)
        load_p(2, 4)
        load_x(2)
        load_scale(3)
        load_x(3)
        load_scale(4)
        load_p(4, 8)
        for c in range(4, NC):
            load_x(c)
            if c + 1 < NC:
                load_scale(c + 1)
        a_bf = keep.tile([P, NG, PACK], BF16, name="a_bf")
        nc.sync.dma_start(out=a_bf[:], in_=a.rearrange("(g m t) -> m g t", g=NG, t=PACK))
        g_bf = keep.tile([P, P], BF16, name="g_bf")
        nc.sync.dma_start(out=g_bf[0:NT, :], in_=g.rearrange("(i p) -> i p", p=P))
        pb1 = {}
        for r in range(WIDE, 2 * PACK):
            pb1[r] = keep.tile([P, D], U8, name="pb1_%d" % r, align_bytes=64)
            nc.sync.dma_start(out=pb1[r][:], in_=p_by[1][:, r - PACK, :])
        for q in range(4):
            nc.sync.dma_start(
                out=vs[32 * q : 32 * q + 4, :, :].bitcast(I32),
                in_=v_scales[:, 4 * q : 4 * q + 4, :].rearrange("g q n -> q g n").bitcast(I32),
            )
        vw = keep.tile([P, NG, 2 * D], U8, name="vw", align_bytes=64)
        for gg in range(NG):
            nc.sync.dma_start(out=vw[:, gg, :].bitcast(I32), in_=v_words[gg].bitcast(I32))
        xn = []
        for j in range(8):
            t = work.tile([P, 4, L], BF16, name="xn_%d" % j, tag="xr", bufs=8, align_bytes=64)
            nc.sync.dma_start(out=t[:], in_=x[512 * j : 512 * (j + 1), :].rearrange("(i p) l -> p i l", p=P))
            xn.append(t)

        xq = keep.tile([P, NC, L], U32, name="xq", align_bytes=64)
        xs = keep.tile([P, NC, L], U8, name="xs", align_bytes=64)
        hq = keep.tile([P, NG, L], U32, name="hq", align_bytes=64)
        hs = keep.tile([P, NG, L], U8, name="hs", align_bytes=64)
        hg1 = keep.tile([P, L, PACK], BF16, name="hg1", align_bytes=64)
        hg0 = keep.tile([P, L, PACK], BF16, name="hg0", align_bytes=64)
        hp0 = keep.tile([P, PACK, L], BF16, name="hp0", align_bytes=64)
        a_f = keep.tile([P, NG * PACK], F32, name="a_f")
        g_f = keep.tile([P, NT], F32, name="g_f")

        W, TR, PG, PQ, PS, XG, ACC = {}, {}, {}, {}, {}, {}, {}

        def product(s, lo, hi):
            units = units_of(s)
            if s not in W:
                W[s] = work.tile([P, WIDE * KP], BF16, name="w", tag="w", align_bytes=64)
            for j in range(lo, hi):
                r, c = units[j]
                if r < PACK:
                    t, off = pb0[c]
                    src = t[:, r, off : off + KP]
                elif r < WIDE:
                    t, off = pb4[c]
                    src = t[:, off : off + KP]
                else:
                    src = pb1[r][:, KP * c : KP * (c + 1)]
                nc.vector.tensor_tensor(
                    out=W[s][:, KP * j : KP * (j + 1)],
                    in0=src.bitcast(E4M3),
                    in1=sc[:, KP * c : KP * (c + 1)],
                    op=MULT,
                )

        def transposes(s, b):
            words = W[s][:].bitcast(F32)
            tr = psum.tile([P, 2, 2, P], F32, name="tr", tag="tr", bufs=8 - WIDE)
            for j in range(2 * b, min(2 * b + 2, len(units_of(s)))):
                for u in range(2):
                    nc.tensor.transpose(tr[:, j % 2, u, :], words[:, 256 * j + u : 256 * (j + 1) : 2], ident[:])
            TR[(s, b)] = tr

        def evac(s, lo, hi):
            if s not in PG:
                PG[s] = work.tile([P, WIDE, P, PACK], BF16, name="pg", tag="pg", align_bytes=64)
            pw = PG[s][:].rearrange("p j m t -> p (j m t)").bitcast(F32)
            pw = pw.rearrange("p (j m u) -> p j m u", j=WIDE, u=2)
            b = lo // 2
            nc.scalar.copy(
                out=pw[:, lo:hi, :, :],
                in_=TR[(s, b)][:, lo - 2 * b : hi - 2 * b, :, :].rearrange("p j u m -> p j m u"),
            )

        def quant_p(s, lo, hi):
            if s not in PQ:
                PQ[s] = work.tile([P, WIDE * P], U32, name="pq", tag="pq", align_bytes=64)
                PS[s] = work.tile([P, WIDE * P], U8, name="ps", tag="ps", align_bytes=64)
            nc.vector.quantize_mx(
                out=PQ[s][:, P * lo : P * hi].bitcast(E4M3X4),
                scales=PS[s][:, P * lo : P * hi],
                in_=PG[s][:, lo:hi, :, :].rearrange("p j m t -> p (j m t)"),
            )

        def x_interleave(c, lo, hi):
            if c not in XG:
                XG[c] = work.tile([P, L, PACK], BF16, name="xg", tag="xg", align_bytes=64)
            nc.scalar.copy(
                out=XG[c][:, lo:hi, :].rearrange("p (c i) t -> p c t i", i=4),
                in_=xr[c][:, :, lo:hi].rearrange("p t (c i) -> p c t i", i=4),
            )

        def quant_x(c):
            nc.vector.quantize_mx(
                out=xq[:, c, :].bitcast(E4M3X4), scales=xs[:, c, :], in_=XG[c][:].rearrange("p l t -> p (l t)")
            )

        def mm(s, lo, hi):
            for j in range(lo, min(hi, len(units_of(s)))):
                r, c = units_of(s)[j]
                if c == 0:
                    ACC[r] = psum.tile([P, L], F32, name="acc", tag="acc", bufs=WIDE)
                nc.tensor.matmul_mx(
                    out=ACC[r][:],
                    lhsT=PQ[s][:, P * j : P * (j + 1)].bitcast(E4M3X4),
                    lhsT_scale=PS[s][:, P * j : P * (j + 1)],
                    rhs=xq[:, c, :].bitcast(E4M3X4),
                    rhs_scale=xs[:, c, :],
                    start=(c == 0),
                    stop=(c == NC - 1),
                )

        def quant_h(gg, src):
            nc.vector.quantize_mx(
                out=hq[:, gg, :].bitcast(E4M3X4), scales=hs[:, gg, :], in_=src[:].rearrange("p l t -> p (l t)")
            )

        def h0_evac(t):
            nc.scalar.activation(out=hp0[:, t, :], in_=ACC[t][:], func=COPY, scale=a_f[:, t : t + 1])

        def h0_interleave(lo, hi):
            nc.scalar.copy(
                out=hg0[:, lo:hi, :].rearrange("p (c i) t -> p c t i", i=4),
                in_=hp0[:, :, lo:hi].rearrange("p t (c i) -> p c t i", i=4),
            )

        def h1_scalar(t, lo, hi):
            r = PACK + t
            nc.scalar.activation(out=hg1[:, lo:hi, t], in_=ACC[r][:, lo:hi], func=COPY, scale=a_f[:, r : r + 1])

        def h1_vector(t, lo, hi):
            r = PACK + t
            nc.vector.tensor_scalar(
                out=hg1[:, lo:hi, t], in0=ACC[r][:, lo:hi], scalar1=a_f[:, r : r + 1], scalar2=None, op0=MULT
            )

        for s in range(STEPS):
            wide = s < NC
            product(s, 0, 2)
            transposes(s, 0)
            if s == NC + 2:
                h0_evac(0)
            if s >= 1:
                n = len(units_of(s - 1))
                evac(s - 1, 4 if n > 4 else 2, n)
            if s == NC + 2:
                h0_evac(1)
            if s == NC + 3:
                h0_evac(2)
                h0_evac(3)
            if wide:
                x_interleave(s, 0, 256)
            evac_late = s == LAST
            if evac_late:
                evac(s, 0, 1)
                evac(s, 1, 2)
            else:
                evac(s, 0, 2)
            if wide:
                x_interleave(s, 256, 512)
            if s == NC + 2:
                h1_scalar(0, 0, 256)
            if s == NC + 3:
                h1_scalar(0, 256, 512)
            if s == NC + 4:
                h0_interleave(0, 512)
            if s == NC + 5:
                h1_scalar(1, 0, 512)
            if s >= 2:
                quant_p(s - 2, 0, 4)
                if s - 2 < NC:
                    quant_p(s - 2, 4, 5)
                mm(s - 2, 0, 2)
            product(s, 2, 4)
            transposes(s, 1)
            if wide:
                evac(s, 2, 4)
            if s >= 2:
                mm(s - 2, 2, 4)
            if wide:
                product(s, 4, 5)
                transposes(s, 2)
                if s >= 2:
                    mm(s - 2, 4, 5)
            elif s - 2 < NC:
                mm(s - 2, 4, 5)
            if 1 <= s <= NC:
                quant_x(s - 1)
            if s == NC + 1:
                nc.scalar.copy(out=a_f[:], in_=a_bf[:].rearrange("p g t -> p (g t)"))
                nc.vector.tensor_copy(out=g_rows[0:NT, :], in_=g_bf[0:NT, :])
        evac(LAST, 2, 3)
        evac(LAST, 3, 4)
        quant_p(LAST - 1, 0, 4)
        mm(LAST - 1, 0, 4)
        for j in range(2):
            quant_p(LAST, j, j + 1)
            mm(LAST, j, j + 1)
        h1_scalar(2, 256, L)
        quant_h(0, hg0)
        h1_vector(2, 0, 256)
        for j in range(2, 4):
            quant_p(LAST, j, j + 1)
            mm(LAST, j, j + 1)
        h1_scalar(3, 256, L)
        h1_vector(3, 0, 256)
        quant_h(1, hg1)

        Y = {}

        def y_pass(i, gg):
            if gg == 0:
                tr = i % 8 < 8 - WIDE
                Y[i] = psum.tile([P, L], F32, name="y", tag="tr" if tr else "acc", bufs=8 - WIDE if tr else WIDE)
            nc.tensor.matmul_mx(
                out=Y[i][:],
                lhsT=vw[:, gg, 256 * i : 256 * (i + 1)].bitcast(E2M1X4),
                lhsT_scale=vs[:, gg, P * i : P * (i + 1)],
                rhs=hq[:, gg, :].bitcast(E4M3X4),
                rhs_scale=hs[:, gg, :],
                start=(gg == 0),
                stop=(gg == NG - 1),
            )

        gt = psum.tile([P, P], F32, name="gt", tag="tr", bufs=8 - WIDE)
        nc.tensor.transpose(gt[:], g_rows[:], ident[:])
        nc.scalar.copy(out=g_f[:], in_=gt[:, 0:NT])

        groups = [(0, 1), (1, 2)] + [(i, i + 2) for i in range(2, NT - 2, 2)] + [(NT - 2, NT - 1), (NT - 1, NT)]
        first, end, o = {}, {}, None
        for lo, hi in groups:
            for i in range(lo, hi):
                first[i], end[i] = lo, hi

        for i in range(7):
            y_pass(i, 0)
        for i in range(NT):
            y_pass(i, 1)
            if i >= 1 and i + 6 < NT:
                y_pass(i + 6, 0)
            if i == first[i]:
                o = work.tile([P, 2, L], F32, name="o", tag="o", bufs=6, align_bytes=64)
            xi, gi, oi = xn[i // 4][:, i % 4, :], g_f[:, i : i + 1], o[:, i - first[i], :]
            if i % 4 == 3 and i < NT - 4:
                gx = work.tile([P, L], F32, name="gx", tag="gx", bufs=2)
                ys = work.tile([P, L], F32, name="ys", tag="ys", bufs=2)
                nc.scalar.activation(out=gx[:], in_=xi, func=COPY, scale=gi)
                nc.scalar.copy(out=ys[:], in_=Y[i][:])
                nc.gpsimd.tensor_tensor(out=oi, in0=gx[:], in1=ys[:], op=SUB)
            else:
                nc.vector.scalar_tensor_tensor(out=oi, in0=xi, scalar=gi, in1=Y[i][:], op0=MULT, op1=SUB)
            if i == end[i] - 1:
                nc.sync.dma_start(
                    out=out[P * first[i] : P * end[i], :].rearrange("(i p) l -> p i l", p=P), in_=o[:, 0 : end[i] - first[i], :]
                )
